import numpy as np
import ml_dtypes


def mxq(x, axis, fmt="e4m3"):
    dtype, down = {"e4m3": (ml_dtypes.float8_e4m3fn, 7), "e5m2": (ml_dtypes.float8_e5m2, 14)}[fmt]
    v = np.moveaxis(np.asarray(x, np.float32).astype(ml_dtypes.bfloat16).astype(np.float64), axis, -1)
    blocks = v.reshape(v.shape[:-1] + (-1, 32))
    amax = np.abs(blocks).max(-1, keepdims=True)
    byte = np.maximum(np.where(amax > 0, np.frexp(amax)[1] - 1 + 127, 0) - down, 1)
    scale = np.exp2(byte - 127.0)
    codes = (blocks / scale).astype(np.float32).astype(dtype).astype(np.float64)
    return np.moveaxis((codes * scale).reshape(v.shape), -1, axis)


WIDE = False


def mx_kscale(k):
    if not WIDE:
        return np.ones(k)
    levels = np.array([10, -10, 5, -5, 0])
    if k % 512:
        return np.exp2(np.random.permutation(np.resize(levels, k // 32))).repeat(32)
    a = np.empty((k // 512, 16))
    for p in range(k // 512):
        a[p, :8] = np.random.permutation(np.resize(levels, 8))
        for g in range(8):
            far = levels[np.abs(levels - a[p, g]) >= 10]
            a[p, g + 8] = far[np.random.randint(len(far))]
    return np.exp2(a.ravel()).repeat(32)


BF16 = ml_dtypes.bfloat16


def bf(x):
    return np.asarray(x, np.float32).astype(BF16)


def f64(x):
    return np.asarray(x).astype(np.float64)


E2M1 = np.array([0.0, 0.5, 1.0, 1.5, 2.0, 3.0, 4.0, 6.0, -0.0, -0.5, -1.0, -1.5, -2.0, -3.0, -4.0, -6.0])


def pack_weight(w, fmt):
    k, n = w.shape
    w = f64(bf(w)).reshape(k // 32, 32, n)
    amax = np.abs(w).max(1)
    if fmt == "e4m3":
        byte = np.frexp(amax)[1] - 1 + 127 - 7
    else:
        mant, ex = np.frexp(amax / 6.0)
        byte = np.where(mant > 0.5, ex, ex - 1) + 127
    byte = np.clip(np.where(amax > 0, byte, 1), 1, 254)
    scaled = (w * np.exp2(127.0 - byte)[:, None, :]).reshape(k, n).astype(np.float32)
    by_word = np.ascontiguousarray(scaled.reshape(k // 512, 128, 4, n).transpose(0, 1, 3, 2))
    if fmt == "e4m3":
        words = by_word.astype(ml_dtypes.float8_e4m3fn).view(np.uint8)
    else:
        c = by_word.astype(ml_dtypes.float4_e2m1fn).view(np.uint8) & 0xF
        words = c[..., 0::2] | (c[..., 1::2] << 4)
    return np.ascontiguousarray(words), np.ascontiguousarray(byte.astype(np.uint8).reshape(k // 512, 16, n))


def unpack_weight(words, scales, fmt):
    g, p, n, _ = words.shape
    if fmt == "e4m3":
        vals = np.ascontiguousarray(words).view(ml_dtypes.float8_e4m3fn).astype(np.float64)
    else:
        nib = np.empty((g, p, n, 4), np.uint8)
        nib[..., 0::2] = words & 0xF
        nib[..., 1::2] = words >> 4
        vals = E2M1[nib]
    vals = vals * np.repeat(np.exp2(scales.astype(np.float64) - 127.0), 8, axis=1)[..., None]
    return vals.transpose(0, 1, 3, 2).reshape(g * 512, n)


T, D, R, V = 1024, 1024, 512, 2048


def unit_ramp(x):
    return np.minimum(1.0, np.maximum(0.0, x))


def draw0():
    s = mx_kscale(D)
    t1 = mx_kscale(R)
    t2 = mx_kscale(R)
    h = np.random.standard_normal((T, D)) * s
    u1 = np.random.standard_normal((D, R)) / np.sqrt(D) / s[:, None] * t1
    u2 = np.random.standard_normal((D, R)) / np.sqrt(D) / s[:, None] * t2
    b1 = (np.random.standard_normal((R, V)) + 0.5 * np.random.standard_normal((R, 1))) / np.sqrt(R) / t1[:, None]
    b2 = 0.7 * np.random.standard_normal((R, V)) / np.sqrt(R) / t2[:, None]
    bias = 0.3 + 0.3 * np.random.standard_normal(V)
    u1_words, u1_scales = pack_weight(u1, "e4m3")
    u2_words, u2_scales = pack_weight(u2, "e4m3")
    b1_words, b1_scales = pack_weight(b1, "e4m3")
    b2_words, b2_scales = pack_weight(b2, "e4m3")
    return {"h": bf(h), "u1_words": u1_words, "u1_scales": u1_scales, "u2_words": u2_words, "u2_scales": u2_scales, "b1_words": b1_words, "b1_scales": b1_scales, "b2_words": b2_words, "b2_scales": b2_scales, "bias": bf(bias)}


def core(h, u1_words, u1_scales, u2_words, u2_scales, b1_words, b1_scales, b2_words, b2_scales, bias):
    hq = mxq(f64(h), 1, "e4m3")
    f1 = hq @ unpack_weight(u1_words, u1_scales, "e4m3")
    f2 = hq @ unpack_weight(u2_words, u2_scales, "e4m3")
    p = (mxq(f1, 1, "e4m3") @ unpack_weight(b1_words, b1_scales, "e4m3")) + f64(bias)[None, :]
    rest = mxq(f2, 1, "e4m3") @ unpack_weight(b2_words, b2_scales, "e4m3")
    mu = np.mean(p, axis=1)
    w = unit_ramp(p - mu[:, None])
    return p + w * rest


def e4m3fn_bytes(y):
    return np.clip(np.asarray(y, np.float64), -448.0, 448.0).astype(np.float32).astype(ml_dtypes.float8_e4m3fn).view(np.uint8)


def e4m3fn_values(b):
    return np.asarray(b, np.uint8).view(ml_dtypes.float8_e4m3fn).astype(np.float64)


def setup_inputs():
    d = draw0()
    x0 = np.asarray(d['h']).astype(np.float64)
    s = (np.max(np.abs(x0), axis=(0,), keepdims=True) / 448.0).astype(np.float32)
    out = {}
    for k, v in d.items():
        if k == 'h':
            out['h_bytes'] = e4m3fn_bytes(x0 / s.astype(np.float64))
            out['h_scale'] = s
        else:
            out[k] = v
    return out


def reference(h_bytes, h_scale, u1_words, u1_scales, u2_words, u2_scales, b1_words, b1_scales, b2_words, b2_scales, bias):
    return core(e4m3fn_values(h_bytes) * h_scale.astype(np.float64), u1_words, u1_scales, u2_words, u2_scales, b1_words, b1_scales, b2_words, b2_scales, bias)

@@ -1,0 +1,288 @@
+from contextlib import ExitStack
+
+import concourse.mybir as mybir
+from concourse.masks import make_identity
+
+T, D, R, V = 1024, 1024, 512, 2048
+FLOPS = 2 * (2 * T * D * R + 2 * T * R * V)
+
+F32 = mybir.dt.float32
+BF16 = mybir.dt.bfloat16
+I32 = mybir.dt.int32
+U8 = mybir.dt.uint8
+FP8 = mybir.dt.float8_e4m3fn
+FP8X4 = mybir.dt.float8_e4m3fn_x4
+ALU = mybir.AluOpType
+ACT = mybir.ActivationFunctionType
+
+P = 128
+PACK = 4
+TILES = T // P
+GROUPS = D // (P * PACK)
+CHUNK = 512
+CHUNKS = V // CHUNK
+HALF = V // 2
+QUADS = 4
+H_COLS = GROUPS * P
+MM_BANKS = 4
+
+
+def tile_previewramprefinedvocablogits_w8_kernel(
+    tc, h_bytes, h_scale, u1_words, u1_scales, u2_words, u2_scales,
+    b1_words, b1_scales, b2_words, b2_scales, bias, out,
+):
+    nc = tc.nc
+    with ExitStack() as ctx:
+        keep = ctx.enter_context(tc.tile_pool(name="keep", bufs=1))
+        psum = ctx.enter_context(tc.psum_pool(name="psum", bufs=1))
+        ctx.enter_context(tc.manual_schedule())
+
+        ident = keep.tile([P, P], F32, name="ident")
+        pick = keep.tile([P, CHUNKS], BF16, name="pick")
+        bias_rows = keep.tile([P, CHUNK], BF16, name="bias_rows")
+        bias_all = keep.tile([P, V], BF16, name="bias_all")
+        hs = keep.tile([P, GROUPS, PACK], F32, name="hs")
+        u_raw = [keep.tile([P, GROUPS, R], I32, name="u_raw%d" % w) for w in range(2)]
+        us_raw = [keep.tile([P, R], U8, name="us_raw%d" % w) for w in range(2)]
+        u_codes = [keep.tile([P, GROUPS, R], I32, name="u_codes%d" % w, align_bytes=64) for w in range(2)]
+        u_planes = [keep.tile([P, R], U8, name="u_planes%d" % w, align_bytes=64) for w in range(2)]
+        b_codes = [keep.tile([P, V], I32, name="b_codes%d" % w, align_bytes=64) for w in range(2)]
+        b_planes = [keep.tile([P, CHUNK], U8, name="b_planes%d" % w, align_bytes=64) for w in range(2)]
+        h_raw = [keep.tile([P, D], U8, name="h_raw%d" % j) for j in range(TILES)]
+
+        for tile in us_raw + b_planes:
+            nc.vector.memset(tile[:].bitcast(I32), 0)
+        nc.gpsimd.memset(bias_rows[:], 0.0)
+        make_identity(nc, ident[:])
+        nc.gpsimd.tensor_copy(out=pick[:], in_=ident[:, 0:CHUNKS])
+
+        def load_h(j):
+            nc.sync.dma_start(out=h_raw[j][:], in_=h_bytes[j * P : (j + 1) * P, :])
+
+        def load_u(w, words, scales):
+            for q in range(QUADS):
+                nc.sync.dma_start(
+                    out=us_raw[w][32 * q : 32 * q + 4 * GROUPS, :].bitcast(I32),
+                    in_=scales[:, 4 * q : 4 * q + 4, :].bitcast(I32),
+                )
+            nc.sync.dma_start(out=u_raw[w][:], in_=words.rearrange("g p n t -> p g (n t)").bitcast(I32))
+
+        def load_b(w, words, scales):
+            for q in range(QUADS):
+                nc.sync.dma_start(
+                    out=b_planes[w][32 * q : 32 * q + 4 * CHUNKS, :].bitcast(I32),
+                    in_=scales[0, 4 * q : 4 * q + 4, :].rearrange("j (c n) -> c j n", c=CHUNKS).bitcast(I32),
+                )
+            nc.sync.dma_start(out=b_codes[w][:], in_=words[0].rearrange("p n t -> p (n t)").bitcast(I32))
+
+        load_h(0)
+        nc.sync.dma_start(out=hs[:], in_=h_scale.rearrange("o (g p t) -> p (o g) t", p=P, t=PACK))
+        load_u(0, u1_words, u1_scales)
+        load_h(1)
+        nc.sync.dma_start(out=bias_rows[0:CHUNKS, :], in_=bias.rearrange("(c n) -> c n", c=CHUNKS))
+        load_u(1, u2_words, u2_scales)
+        load_h(2)
+        load_b(0, b1_words, b1_scales)
+        load_h(3)
+        load_b(1, b2_words, b2_scales)
+        for j in range(4, TILES):
+            load_h(j)
+
+        wide, turned, f_banks, stage, codes, planes, prev, ramp, sums, banks = ({} for i in range(10))
+        bank_count = [0]
+
+        def next_bank(shape, dtype):
+            n = bank_count[0]
+            bank_count.append(n + 1)
+            bank_count.remove(n)
+            return psum.tile(shape, dtype, name="mm", tag="mm%d" % (n % MM_BANKS))
+
+        def stage_tiles(s):
+            if s not in stage:
+                stage[s] = keep.tile([P, 2 * D], BF16, name="stage", tag="stage%d" % (s % 3), align_bytes=64)
+                codes[s] = keep.tile([P, 2 * H_COLS], I32, name="codes", tag="codes%d" % (s % 4), align_bytes=64)
+                planes[s] = keep.tile([P, 2 * H_COLS], U8, name="planes", tag="planes%d" % (s % 4), align_bytes=64)
+            return stage[s]
+
+        def permute_scales(w):
+            nc.vector.tensor_copy(
+                out=u_planes[w][:].rearrange("p (t a b) -> p a t b", t=PACK, b=16),
+                in_=us_raw[w][:].rearrange("p (a b t) -> p a t b", t=PACK, b=16),
+            )
+
+        def permute_words(w):
+            nc.vector.tensor_copy(
+                out=u_codes[w][:].rearrange("p g (t a b) -> p g a t b", t=PACK, b=4),
+                in_=u_raw[w][:].rearrange("p g (a b t) -> p g a t b", t=PACK, b=4),
+            )
+
+        def spread_bias():
+            for half in range(2):
+                bank = next_bank([P, HALF], BF16)
+                for i in range(2):
+                    c = 2 * half + i
+                    nc.tensor.matmul(
+                        bank[:, i * CHUNK : (i + 1) * CHUNK],
+                        lhsT=pick[:, c : c + 1].to_broadcast([P, P]),
+                        rhs=bias_rows[:],
+                        start=True,
+                        stop=True,
+                    )
+                nc.scalar.copy(out=bias_all[:, half * HALF : (half + 1) * HALF], in_=bank[:])
+
+        def widen(j):
+            wide[j] = keep.tile([P, D], BF16, name="wide", tag="wide%d" % (j % 2))
+            if j == 0:
+                nc.vector.tensor_copy(out=wide[j][:], in_=h_raw[j][:].bitcast(FP8))
+            else:
+                nc.scalar.copy(out=wide[j][:], in_=h_raw[j][:].bitcast(FP8))
+
+        def turn(j):
+            turned[j] = psum.tile([P, 2, GROUPS, P], F32, name="turned", tag="turned%d" % (j % 2))
+            pairs = wide[j][:].bitcast(F32)
+            for g in range(GROUPS):
+                for u in range(2):
+                    nc.tensor.transpose(turned[j][:, u, g, :], pairs[:, 256 * g + u : 256 * (g + 1) : 2], ident[:])
+
+        def scale_h(j):
+            dst = stage_tiles(j - 3)
+            src = turned[j][:].rearrange("p u g n -> p (u g n)").bitcast(BF16)
+            nc.vector.tensor_tensor(
+                out=dst[:, 0:D].rearrange("p (g n u e) -> p g n u e", g=GROUPS, u=2, e=2),
+                in0=src.rearrange("p (u g n e) -> p g n u e", u=2, g=GROUPS, e=2),
+                in1=hs[:].rearrange("p g (u e) -> p g u e", u=2).unsqueeze(2).to_broadcast([P, GROUPS, P, 2, 2]),
+                op=ALU.mult,
+            )
+
+        def quantize(s, lo, hi):
+            nc.vector.quantize_mx(
+                out=codes[s][:, lo:hi].bitcast(FP8X4),
+                scales=planes[s][:, lo:hi],
+                in_=stage[s][:, PACK * lo : PACK * hi],
+            )
+
+        def project(j):
+            dst = stage_tiles(j - 2)
+            for w in range(2):
+                bank = psum.tile([P, PACK, P], F32, name="f_bank", tag="f_bank%d" % w)
+                for t in range(PACK):
+                    cols = slice(t * P, (t + 1) * P)
+                    for g in range(GROUPS):
+                        nc.tensor.matmul_mx(
+                            out=bank[:, t, :],
+                            lhsT=u_codes[w][:, g, cols].bitcast(FP8X4),
+                            lhsT_scale=u_planes[w][4 * g :, cols],
+                            rhs=codes[j - 3][:, g * P : (g + 1) * P].bitcast(FP8X4),
+                            rhs_scale=planes[j - 3][:, g * P : (g + 1) * P],
+                            start=(g == 0),
+                            stop=(g == GROUPS - 1),
+                        )
+                nc.scalar.copy(
+                    out=dst[:, D + w * R : D + (w + 1) * R].rearrange("p (n t) -> p n t", t=PACK),
+                    in_=bank[:].rearrange("p t n -> p n t"),
+                )
+
+        def logits(w, j, c):
+            banks[w, j, c] = next_bank([P, CHUNK], F32)
+            cols = slice(H_COLS + w * P, H_COLS + (w + 1) * P)
+            nc.tensor.matmul_mx(
+                out=banks[w, j, c][:],
+                lhsT=codes[j - 2][:, cols].bitcast(FP8X4),
+                lhsT_scale=planes[j - 2][:, cols],
+                rhs=b_codes[w][:, c * CHUNK : (c + 1) * CHUNK].bitcast(FP8X4),
+                rhs_scale=b_planes[w][4 * c :, :],
+                start=True,
+                stop=True,
+            )
+
+        def add_bias(j, c):
+            if c == 0:
+                prev[j] = keep.tile([P, V], F32, name="prev", tag="prev%d" % (j % 3))
+                sums[j] = keep.tile([P, CHUNKS], F32, name="sums", tag="sums%d" % (j % 2))
+            cols = slice(c * CHUNK, (c + 1) * CHUNK)
+            nc.vector.scalar_tensor_tensor(
+                out=prev[j][:, cols], in0=banks[0, j, c][:], scalar=1.0, in1=bias_all[:, cols],
+                op0=ALU.mult, op1=ALU.add, accum_out=sums[j][:, c : c + 1],
+            )
+
+        def rectify(j):
+            parts = keep.tile([P, CHUNKS], F32, name="parts", tag="parts%d" % (j % 2))
+            neg_mu = keep.tile([P, 1], F32, name="neg_mu", tag="neg_mu%d" % (j % 2))
+            nc.scalar.activation(out=parts[:], in_=sums[j][:], func=ACT.Copy, scale=-1.0 / V, accum_out=neg_mu[:])
+            ramp[j] = keep.tile([P, V], F32, name="ramp", tag="ramp%d" % (j % 4))
+            for half in range(2):
+                cols = slice(half * HALF, (half + 1) * HALF)
+                nc.scalar.activation(out=ramp[j][:, cols], in_=prev[j][:, cols], func=ACT.Relu, bias=neg_mu[:])
+
+        def weigh(j, c):
+            cols = slice(c * CHUNK, (c + 1) * CHUNK)
+            nc.vector.scalar_tensor_tensor(
+                out=ramp[j][:, cols], in0=ramp[j][:, cols], scalar=1.0, in1=banks[1, j, c][:],
+                op0=ALU.min, op1=ALU.mult,
+            )
+
+        def finish(engine, j, cols):
+            engine.tensor_tensor(out=ramp[j][:, cols], in0=prev[j][:, cols], in1=ramp[j][:, cols], op=ALU.add)
+            nc.sync.dma_start(out=out[j * P : (j + 1) * P, cols], in_=ramp[j][:, cols])
+
+        widen(0)
+        turn(0)
+        permute_scales(0)
+        permute_words(0)
+        widen(1)
+        turn(1)
+        spread_bias()
+        scale_h(0)
+        permute_scales(1)
+        quantize(-3, 0, H_COLS)
+        permute_words(1)
+        project(0)
+        scale_h(1)
+        quantize(-2, H_COLS, 2 * H_COLS)
+        quantize(-2, 0, H_COLS)
+
+        last = TILES - 1
+        for s in range(-1, TILES):
+            now, nxt = s >= 0, s + 1 <= last
+            if s + 3 <= last:
+                widen(s + 3)
+            if now:
+                logits(1, s, 0)
+                logits(1, s, 1)
+            if nxt:
+                logits(0, s + 1, 0)
+                logits(0, s + 1, 1)
+            if s + 2 <= last:
+                project(s + 2)
+            if now:
+                weigh(s, 0)
+                weigh(s, 1)
+                if s < last:
+                    finish(nc.gpsimd, s, slice(0, HALF))
+            if nxt:
+                logits(0, s + 1, 2)
+                logits(0, s + 1, 3)
+            if s + 3 <= last:
+                turn(s + 3)
+            if nxt:
+                add_bias(s + 1, 0)
+                add_bias(s + 1, 1)
+            if now:
+                logits(1, s, 2)
+                logits(1, s, 3)
+            if nxt:
+                add_bias(s + 1, 2)
+                add_bias(s + 1, 3)
+                rectify(s + 1)
+            if s + 3 <= last:
+                scale_h(s + 3)
+            if now:
+                weigh(s, 2)
+            if s + 2 <= last:
+                quantize(s, 0 if s + 3 <= last else H_COLS, 2 * H_COLS)
+            if now:
+                weigh(s, 3)
+                if s < last:
+                    finish(nc.gpsimd, s, slice(HALF, V))
+        for c in range(CHUNKS):
+            finish(nc.vector, last, slice(c * CHUNK, (c + 1) * CHUNK))

@@ -24,7 +24,11 @@ CHUNKS = V // CHUNK
 HALF = V // 2
 QUADS = 4
 H_COLS = GROUPS * P
-MM_BANKS = 4
+VEC_BANKS = 5
+ACT_BANKS = 3
+H_LEAD, F_LEAD = 4, 2
+VEC_WIDENS = 2
+SPREAD = CHUNKS - 1
 
 
 def tile_previewramprefinedvocablogits_w8_kernel(
@@ -40,68 +44,80 @@ def tile_previewramprefinedvocablogits_w8_kernel(
         ident = keep.tile([P, P], F32, name="ident")
         pick = keep.tile([P, CHUNKS], BF16, name="pick")
         bias_rows = keep.tile([P, CHUNK], BF16, name="bias_rows")
-        bias_all = keep.tile([P, V], BF16, name="bias_all")
+        bias_all = keep.tile([P, SPREAD * CHUNK], BF16, name="bias_all")
         hs = keep.tile([P, GROUPS, PACK], F32, name="hs")
         u_raw = [keep.tile([P, GROUPS, R], I32, name="u_raw%d" % w) for w in range(2)]
-        us_raw = [keep.tile([P, R], U8, name="us_raw%d" % w) for w in range(2)]
+        zeroed = keep.tile([P, 4 * CHUNK], U8, name="zeroed", align_bytes=64)
+        us_raw = [zeroed[:, w * R : (w + 1) * R] for w in range(2)]
         u_codes = [keep.tile([P, GROUPS, R], I32, name="u_codes%d" % w, align_bytes=64) for w in range(2)]
         u_planes = [keep.tile([P, R], U8, name="u_planes%d" % w, align_bytes=64) for w in range(2)]
         b_codes = [keep.tile([P, V], I32, name="b_codes%d" % w, align_bytes=64) for w in range(2)]
-        b_planes = [keep.tile([P, CHUNK], U8, name="b_planes%d" % w, align_bytes=64) for w in range(2)]
+        b_planes = [zeroed[:, 2 * R + w * CHUNK : 2 * R + (w + 1) * CHUNK] for w in range(2)]
         h_raw = [keep.tile([P, D], U8, name="h_raw%d" % j) for j in range(TILES)]
 
-        for tile in us_raw + b_planes:
-            nc.vector.memset(tile[:].bitcast(I32), 0)
-        nc.gpsimd.memset(bias_rows[:], 0.0)
-        make_identity(nc, ident[:])
-        nc.gpsimd.tensor_copy(out=pick[:], in_=ident[:, 0:CHUNKS])
+        nc.vector.memset(zeroed[:].bitcast(I32), 0)
+        nc.vector.memset(ident[:], 0.0)
+        nc.vector.memset(bias_rows[:], 0.0)
+        make_identity(nc, ident[:], nomemset=True)
+        nc.scalar.copy(out=pick[:], in_=ident[:, 0:CHUNKS])
 
         def load_h(j):
             nc.sync.dma_start(out=h_raw[j][:], in_=h_bytes[j * P : (j + 1) * P, :])
 
-        def load_u(w, words, scales):
+        def load_u_scales(w, scales):
             for q in range(QUADS):
                 nc.sync.dma_start(
                     out=us_raw[w][32 * q : 32 * q + 4 * GROUPS, :].bitcast(I32),
                     in_=scales[:, 4 * q : 4 * q + 4, :].bitcast(I32),
                 )
+
+        def load_u_words(w, words):
             nc.sync.dma_start(out=u_raw[w][:], in_=words.rearrange("g p n t -> p g (n t)").bitcast(I32))
 
-        def load_b(w, words, scales):
+        def load_b_scales(w, scales):
             for q in range(QUADS):
                 nc.sync.dma_start(
                     out=b_planes[w][32 * q : 32 * q + 4 * CHUNKS, :].bitcast(I32),
                     in_=scales[0, 4 * q : 4 * q + 4, :].rearrange("j (c n) -> c j n", c=CHUNKS).bitcast(I32),
                 )
-            nc.sync.dma_start(out=b_codes[w][:], in_=words[0].rearrange("p n t -> p (n t)").bitcast(I32))
+
+        def load_b_words(w, words, half):
+            cols = slice(half * HALF, (half + 1) * HALF)
+            nc.sync.dma_start(out=b_codes[w][:, cols], in_=words[0].rearrange("p n t -> p (n t)").bitcast(I32)[:, cols])
 
         load_h(0)
-        nc.sync.dma_start(out=hs[:], in_=h_scale.rearrange("o (g p t) -> p (o g) t", p=P, t=PACK))
-        load_u(0, u1_words, u1_scales)
         load_h(1)
+        load_u_words(0, u1_words)
+        nc.sync.dma_start(out=hs[:], in_=h_scale.rearrange("o (g p t) -> p (o g) t", p=P, t=PACK))
+        load_u_scales(0, u1_scales)
         nc.sync.dma_start(out=bias_rows[0:CHUNKS, :], in_=bias.rearrange("(c n) -> c n", c=CHUNKS))
-        load_u(1, u2_words, u2_scales)
         load_h(2)
-        load_b(0, b1_words, b1_scales)
+        load_u_words(1, u2_words)
         load_h(3)
-        load_b(1, b2_words, b2_scales)
-        for j in range(4, TILES):
+        load_u_scales(1, u2_scales)
+        load_b_words(0, b1_words, 1)
+        load_b_scales(0, b1_scales)
+        load_b_words(0, b1_words, 0)
+        load_h(4)
+        load_b_scales(1, b2_scales)
+        load_b_words(1, b2_words, 0)
+        load_b_words(1, b2_words, 1)
+        for j in range(5, TILES):
             load_h(j)
 
         wide, turned, f_banks, stage, codes, planes, prev, ramp, sums, banks = ({} for i in range(10))
-        bank_count = [0]
+        across, parked, back, neg_mu = {}, {}, {}, {}
+        taken = []
 
         def next_bank(shape, dtype):
-            n = bank_count[0]
-            bank_count.append(n + 1)
-            bank_count.remove(n)
-            return psum.tile(shape, dtype, name="mm", tag="mm%d" % (n % MM_BANKS))
+            taken.append(len(taken))
+            return psum.tile(shape, dtype, name="bank", tag="ring%d" % (taken[-1] % VEC_BANKS))
 
         def stage_tiles(s):
             if s not in stage:
-                stage[s] = keep.tile([P, 2 * D], BF16, name="stage", tag="stage%d" % (s % 3), align_bytes=64)
-                codes[s] = keep.tile([P, 2 * H_COLS], I32, name="codes", tag="codes%d" % (s % 4), align_bytes=64)
-                planes[s] = keep.tile([P, 2 * H_COLS], U8, name="planes", tag="planes%d" % (s % 4), align_bytes=64)
+                stage[s] = keep.tile([P, 2 * D], BF16, name="stage", tag="stage%d" % (s % 4), align_bytes=64)
+                codes[s] = keep.tile([P, 2 * H_COLS], I32, name="codes", tag="codes%d" % (s % 5), align_bytes=64)
+                planes[s] = keep.tile([P, 2 * H_COLS], U8, name="planes", tag="planes%d" % (s % 5), align_bytes=64)
             return stage[s]
 
         def permute_scales(w):
@@ -116,36 +132,35 @@ def tile_previewramprefinedvocablogits_w8_kernel(
                 in_=u_raw[w][:].rearrange("p g (a b t) -> p g a t b", t=PACK, b=4),
             )
 
+        def bias_matmul(dst, c, stop):
+            nc.tensor.matmul(
+                dst, lhsT=pick[:, c : c + 1].to_broadcast([P, P]), rhs=bias_rows[:], start=True, stop=stop
+            )
+
         def spread_bias():
-            for half in range(2):
-                bank = next_bank([P, HALF], BF16)
-                for i in range(2):
-                    c = 2 * half + i
-                    nc.tensor.matmul(
-                        bank[:, i * CHUNK : (i + 1) * CHUNK],
-                        lhsT=pick[:, c : c + 1].to_broadcast([P, P]),
-                        rhs=bias_rows[:],
-                        start=True,
-                        stop=True,
-                    )
-                nc.scalar.copy(out=bias_all[:, half * HALF : (half + 1) * HALF], in_=bank[:])
+            for first in range(0, SPREAD, 2):
+                n = min(2, SPREAD - first)
+                bank = psum.tile([P, n * CHUNK], BF16, name="spread", tag="f_bank%d" % (first // 2))
+                for i in range(n):
+                    bias_matmul(bank[:, i * CHUNK : (i + 1) * CHUNK], first + i, True)
+                nc.scalar.copy(out=bias_all[:, first * CHUNK : (first + n) * CHUNK], in_=bank[:])
 
         def widen(j):
-            wide[j] = keep.tile([P, D], BF16, name="wide", tag="wide%d" % (j % 2))
-            if j == 0:
+            wide[j] = keep.tile([P, D], BF16, name="wide", tag="wide%d" % (j % 3))
+            if j < VEC_WIDENS:
                 nc.vector.tensor_copy(out=wide[j][:], in_=h_raw[j][:].bitcast(FP8))
             else:
                 nc.scalar.copy(out=wide[j][:], in_=h_raw[j][:].bitcast(FP8))
 
         def turn(j):
-            turned[j] = psum.tile([P, 2, GROUPS, P], F32, name="turned", tag="turned%d" % (j % 2))
+            turned[j] = next_bank([P, 2, GROUPS, P], F32)
             pairs = wide[j][:].bitcast(F32)
             for g in range(GROUPS):
                 for u in range(2):
                     nc.tensor.transpose(turned[j][:, u, g, :], pairs[:, 256 * g + u : 256 * (g + 1) : 2], ident[:])
 
         def scale_h(j):
-            dst = stage_tiles(j - 3)
+            dst = stage_tiles(j - H_LEAD)
             src = turned[j][:].rearrange("p u g n -> p (u g n)").bitcast(BF16)
             nc.vector.tensor_tensor(
                 out=dst[:, 0:D].rearrange("p (g n u e) -> p g n u e", g=GROUPS, u=2, e=2),
@@ -161,34 +176,77 @@ def tile_previewramprefinedvocablogits_w8_kernel(
                 in_=stage[s][:, PACK * lo : PACK * hi],
             )
 
-        def project(j):
-            dst = stage_tiles(j - 2)
-            for w in range(2):
-                bank = psum.tile([P, PACK, P], F32, name="f_bank", tag="f_bank%d" % w)
-                for t in range(PACK):
-                    cols = slice(t * P, (t + 1) * P)
-                    for g in range(GROUPS):
-                        nc.tensor.matmul_mx(
-                            out=bank[:, t, :],
-                            lhsT=u_codes[w][:, g, cols].bitcast(FP8X4),
-                            lhsT_scale=u_planes[w][4 * g :, cols],
-                            rhs=codes[j - 3][:, g * P : (g + 1) * P].bitcast(FP8X4),
-                            rhs_scale=planes[j - 3][:, g * P : (g + 1) * P],
-                            start=(g == 0),
-                            stop=(g == GROUPS - 1),
-                        )
-                nc.scalar.copy(
-                    out=dst[:, D + w * R : D + (w + 1) * R].rearrange("p (n t) -> p n t", t=PACK),
-                    in_=bank[:].rearrange("p t n -> p n t"),
+        def project(j, w):
+            bank = psum.tile([P, PACK, P], F32, name="f_bank", tag="f_bank%d" % w)
+            f_banks[j, w] = bank
+            for t in range(PACK):
+                cols = slice(t * P, (t + 1) * P)
+                for g in range(GROUPS):
+                    nc.tensor.matmul_mx(
+                        out=bank[:, t, :],
+                        lhsT=u_codes[w][:, g, cols].bitcast(FP8X4),
+                        lhsT_scale=u_planes[w][4 * g :, cols],
+                        rhs=codes[j - H_LEAD][:, g * P : (g + 1) * P].bitcast(FP8X4),
+                        rhs_scale=planes[j - H_LEAD][:, g * P : (g + 1) * P],
+                        start=(g == 0),
+                        stop=(g == GROUPS - 1),
+                    )
+
+        def round_f(j, w):
+            dst = stage_tiles(j - F_LEAD)
+            nc.scalar.copy(
+                out=dst[:, D + w * R : D + (w + 1) * R].rearrange("p (n t) -> p n t", t=PACK),
+                in_=f_banks[j, w][:].rearrange("p t n -> p n t"),
+            )
+
+        def logits_turned(j):
+            c = SPREAD
+            across[j] = psum.tile([P, CHUNK], F32, name="across", tag="detour")
+            cols = slice(H_COLS, H_COLS + P)
+            for i in range(CHUNK // P):
+                nc.tensor.matmul_mx(
+                    out=across[j][:, i * P : (i + 1) * P],
+                    lhsT=b_codes[0][:, c * CHUNK + i * P : c * CHUNK + (i + 1) * P].bitcast(FP8X4),
+                    lhsT_scale=b_planes[0][4 * c :, i * P : (i + 1) * P],
+                    rhs=codes[j - F_LEAD][:, cols].bitcast(FP8X4),
+                    rhs_scale=planes[j - F_LEAD][:, cols],
+                    start=True,
+                    stop=True,
                 )
+
+        def park_turned(j):
+            parked[j] = keep.tile([P, CHUNK], F32, name="parked", tag="parked%d" % (j % 2))
+            nc.scalar.copy(out=parked[j][:], in_=across[j][:])
+
+        def turn_back(j):
+            back[j] = psum.tile([P, CHUNK], F32, name="back", tag="detour")
+            bias_matmul(back[j][:], SPREAD, False)
+            for i in range(CHUNK // P):
+                cols = slice(i * P, (i + 1) * P)
+                nc.tensor.matmul(
+                    back[j][:, cols], lhsT=parked[j][:, cols], rhs=ident[:], is_transpose=True,
+                    start=False, stop=(i == CHUNK // P - 1),
+                )
+
+        def preview_tiles(j):
+            if j not in prev:
+                prev[j] = keep.tile([P, V], F32, name="prev", tag="prev%d" % (j % 3))
+                sums[j] = keep.tile([P, CHUNKS], F32, name="sums", tag="sums%d" % (j % 2))
+
+        def empty_back(j):
+            preview_tiles(j)
+            nc.scalar.activation(
+                out=prev[j][:, SPREAD * CHUNK :], in_=back[j][:], func=ACT.Copy,
+                accum_out=sums[j][:, SPREAD : SPREAD + 1],
+            )
 
         def logits(w, j, c):
             banks[w, j, c] = next_bank([P, CHUNK], F32)
             cols = slice(H_COLS + w * P, H_COLS + (w + 1) * P)
             nc.tensor.matmul_mx(
                 out=banks[w, j, c][:],
-                lhsT=codes[j - 2][:, cols].bitcast(FP8X4),
-                lhsT_scale=planes[j - 2][:, cols],
+                lhsT=codes[j - F_LEAD][:, cols].bitcast(FP8X4),
+                lhsT_scale=planes[j - F_LEAD][:, cols],
                 rhs=b_codes[w][:, c * CHUNK : (c + 1) * CHUNK].bitcast(FP8X4),
                 rhs_scale=b_planes[w][4 * c :, :],
                 start=True,
@@ -196,23 +254,22 @@ def tile_previewramprefinedvocablogits_w8_kernel(
             )
 
         def add_bias(j, c):
-            if c == 0:
-                prev[j] = keep.tile([P, V], F32, name="prev", tag="prev%d" % (j % 3))
-                sums[j] = keep.tile([P, CHUNKS], F32, name="sums", tag="sums%d" % (j % 2))
+            preview_tiles(j)
             cols = slice(c * CHUNK, (c + 1) * CHUNK)
             nc.vector.scalar_tensor_tensor(
                 out=prev[j][:, cols], in0=banks[0, j, c][:], scalar=1.0, in1=bias_all[:, cols],
                 op0=ALU.mult, op1=ALU.add, accum_out=sums[j][:, c : c + 1],
             )
 
-        def rectify(j):
+        def row_mean(j):
             parts = keep.tile([P, CHUNKS], F32, name="parts", tag="parts%d" % (j % 2))
-            neg_mu = keep.tile([P, 1], F32, name="neg_mu", tag="neg_mu%d" % (j % 2))
-            nc.scalar.activation(out=parts[:], in_=sums[j][:], func=ACT.Copy, scale=-1.0 / V, accum_out=neg_mu[:])
+            neg_mu[j] = keep.tile([P, 1], F32, name="neg_mu", tag="neg_mu%d" % (j % 2))
+            nc.scalar.activation(out=parts[:], in_=sums[j][:], func=ACT.Copy, scale=-1.0 / V, accum_out=neg_mu[j][:])
             ramp[j] = keep.tile([P, V], F32, name="ramp", tag="ramp%d" % (j % 4))
-            for half in range(2):
-                cols = slice(half * HALF, (half + 1) * HALF)
-                nc.scalar.activation(out=ramp[j][:, cols], in_=prev[j][:, cols], func=ACT.Relu, bias=neg_mu[:])
+
+        def rectify(j, half):
+            cols = slice(half * HALF, (half + 1) * HALF)
+            nc.scalar.activation(out=ramp[j][:, cols], in_=prev[j][:, cols], func=ACT.Relu, bias=neg_mu[j][:])
 
         def weigh(j, c):
             cols = slice(c * CHUNK, (c + 1) * CHUNK)
@@ -227,62 +284,101 @@ def tile_previewramprefinedvocablogits_w8_kernel(
 
         widen(0)
         turn(0)
-        permute_scales(0)
-        permute_words(0)
         widen(1)
         turn(1)
+        permute_words(0)
+        widen(2)
         spread_bias()
         scale_h(0)
-        permute_scales(1)
-        quantize(-3, 0, H_COLS)
-        permute_words(1)
-        project(0)
+        permute_scales(0)
+        quantize(-4, 0, H_COLS)
+        project(0, 0)
+        round_f(0, 0)
+        turn(2)
+        widen(3)
         scale_h(1)
-        quantize(-2, H_COLS, 2 * H_COLS)
+        permute_words(1)
+        quantize(-3, 0, H_COLS)
+        permute_scales(1)
+        quantize(-2, H_COLS, H_COLS + P)
+        project(1, 0)
+        project(0, 1)
+        round_f(1, 0)
+        round_f(0, 1)
+        logits_turned(0)
+        park_turned(0)
+        logits(0, 0, 2)
+        project(1, 1)
+        logits(0, 0, 0)
+        logits(0, 0, 1)
+        scale_h(2)
+        quantize(-1, H_COLS, H_COLS + P)
         quantize(-2, 0, H_COLS)
+        quantize(-2, H_COLS + P, 2 * H_COLS)
+        turn_back(0)
+        turn(3)
+        round_f(1, 1)
+        empty_back(0)
+        for c in (2, 0, 1):
+            add_bias(0, c)
+        row_mean(0)
+        rectify(0, 0)
+        widen(4)
+        quantize(-1, H_COLS + P, 2 * H_COLS)
+        scale_h(3)
+        logits(1, 0, 0)
+        logits(1, 0, 1)
+        project(2, 0)
+        project(2, 1)
 
         last = TILES - 1
-        for s in range(-1, TILES):
-            now, nxt = s >= 0, s + 1 <= last
-            if s + 3 <= last:
-                widen(s + 3)
-            if now:
-                logits(1, s, 0)
-                logits(1, s, 1)
+        for s in range(TILES):
+            nxt = s + 1 <= last
             if nxt:
                 logits(0, s + 1, 0)
+                logits_turned(s + 1)
                 logits(0, s + 1, 1)
-            if s + 2 <= last:
-                project(s + 2)
-            if now:
-                weigh(s, 0)
-                weigh(s, 1)
-                if s < last:
-                    finish(nc.gpsimd, s, slice(0, HALF))
-            if nxt:
                 logits(0, s + 1, 2)
-                logits(0, s + 1, 3)
-            if s + 3 <= last:
-                turn(s + 3)
+            rectify(s, 1)
+            weigh(s, 0)
+            weigh(s, 1)
+            if s == 0:
+                quantize(-1, 0, H_COLS)
+            if s < last:
+                finish(nc.gpsimd, s, slice(0, HALF))
+            if s + H_LEAD <= last:
+                turn(s + H_LEAD)
+            if nxt:
+                park_turned(s + 1)
+                turn_back(s + 1)
+            if s + F_LEAD <= last:
+                round_f(s + F_LEAD, 0)
+                round_f(s + F_LEAD, 1)
+            if nxt:
+                empty_back(s + 1)
+            logits(1, s, 2)
             if nxt:
                 add_bias(s + 1, 0)
-                add_bias(s + 1, 1)
-            if now:
-                logits(1, s, 2)
-                logits(1, s, 3)
+            logits(1, s, 3)
+            if s + F_LEAD + 1 <= last:
+                project(s + F_LEAD + 1, 0)
+                project(s + F_LEAD + 1, 1)
             if nxt:
+                add_bias(s + 1, 1)
+                logits(1, s + 1, 0)
                 add_bias(s + 1, 2)
-                add_bias(s + 1, 3)
-                rectify(s + 1)
-            if s + 3 <= last:
-                scale_h(s + 3)
-            if now:
-                weigh(s, 2)
-            if s + 2 <= last:
-                quantize(s, 0 if s + 3 <= last else H_COLS, 2 * H_COLS)
-            if now:
-                weigh(s, 3)
-                if s < last:
-                    finish(nc.gpsimd, s, slice(HALF, V))
+                logits(1, s + 1, 1)
+                row_mean(s + 1)
+                rectify(s + 1, 0)
+            if s + H_LEAD + 1 <= last:
+                widen(s + H_LEAD + 1)
+            if s + H_LEAD <= last:
+                scale_h(s + H_LEAD)
+            weigh(s, 2)
+            weigh(s, 3)
+            if s + F_LEAD <= last:
+                quantize(s, 0 if s + H_LEAD <= last else H_COLS, 2 * H_COLS)
+            if s < last:
+                finish(nc.gpsimd, s, slice(HALF, V))
         for c in range(CHUNKS):
             finish(nc.vector, last, slice(c * CHUNK, (c + 1) * CHUNK))

@@ -26,7 +26,7 @@ QUADS = 4
 H_COLS = GROUPS * P
 VEC_BANKS = 5
 ACT_BANKS = 3
-H_LEAD, F_LEAD = 4, 2
+H_LEAD, F_LEAD = 4, 3
 VEC_WIDENS = 2
 SPREAD = CHUNKS - 1
 
@@ -53,7 +53,7 @@ def tile_previewramprefinedvocablogits_w8_kernel(
         u_planes = [keep.tile([P, R], U8, name="u_planes%d" % w, align_bytes=64) for w in range(2)]
         b_codes = [keep.tile([P, V], I32, name="b_codes%d" % w, align_bytes=64) for w in range(2)]
         b_planes = [zeroed[:, 2 * R + w * CHUNK : 2 * R + (w + 1) * CHUNK] for w in range(2)]
-        h_raw = [keep.tile([P, D], U8, name="h_raw%d" % j) for j in range(TILES)]
+        h_raw = keep.tile([P, TILES, D], U8, name="h_raw")
 
         nc.vector.memset(zeroed[:].bitcast(I32), 0)
         nc.vector.memset(ident[:], 0.0)
@@ -61,8 +61,9 @@ def tile_previewramprefinedvocablogits_w8_kernel(
         make_identity(nc, ident[:], nomemset=True)
         nc.scalar.copy(out=pick[:], in_=ident[:, 0:CHUNKS])
 
-        def load_h(j):
-            nc.sync.dma_start(out=h_raw[j][:], in_=h_bytes[j * P : (j + 1) * P, :])
+        def load_h(first, stop):
+            rows = h_bytes[first * P : stop * P, :]
+            nc.sync.dma_start(out=h_raw[:, first:stop, :], in_=rows.rearrange("(j p) d -> p j d", p=P))
 
         def load_u_scales(w, scales):
             for q in range(QUADS):
@@ -85,28 +86,25 @@ def tile_previewramprefinedvocablogits_w8_kernel(
             cols = slice(half * HALF, (half + 1) * HALF)
             nc.sync.dma_start(out=b_codes[w][:, cols], in_=words[0].rearrange("p n t -> p (n t)").bitcast(I32)[:, cols])
 
-        load_h(0)
-        load_h(1)
-        load_u_words(0, u1_words)
+        load_h(0, 1)
         nc.sync.dma_start(out=hs[:], in_=h_scale.rearrange("o (g p t) -> p (o g) t", p=P, t=PACK))
+        load_h(1, 4)
+        load_u_words(0, u1_words)
         load_u_scales(0, u1_scales)
         nc.sync.dma_start(out=bias_rows[0:CHUNKS, :], in_=bias.rearrange("(c n) -> c n", c=CHUNKS))
-        load_h(2)
+        load_h(4, 6)
         load_u_words(1, u2_words)
-        load_h(3)
         load_u_scales(1, u2_scales)
         load_b_words(0, b1_words, 1)
         load_b_scales(0, b1_scales)
         load_b_words(0, b1_words, 0)
-        load_h(4)
         load_b_scales(1, b2_scales)
         load_b_words(1, b2_words, 0)
+        load_h(6, 8)
         load_b_words(1, b2_words, 1)
-        for j in range(5, TILES):
-            load_h(j)
 
         wide, turned, f_banks, stage, codes, planes, prev, ramp, sums, banks = ({} for i in range(10))
-        across, parked, back, neg_mu = {}, {}, {}, {}
+        across, parked, back, neg_mu, spread = {}, {}, {}, {}, {}
         taken = []
 
         def next_bank(shape, dtype):
@@ -137,20 +135,22 @@ def tile_previewramprefinedvocablogits_w8_kernel(
                 dst, lhsT=pick[:, c : c + 1].to_broadcast([P, P]), rhs=bias_rows[:], start=True, stop=stop
             )
 
-        def spread_bias():
-            for first in range(0, SPREAD, 2):
-                n = min(2, SPREAD - first)
-                bank = psum.tile([P, n * CHUNK], BF16, name="spread", tag="f_bank%d" % (first // 2))
-                for i in range(n):
-                    bias_matmul(bank[:, i * CHUNK : (i + 1) * CHUNK], first + i, True)
-                nc.scalar.copy(out=bias_all[:, first * CHUNK : (first + n) * CHUNK], in_=bank[:])
+        def spread_bias(first):
+            n = min(2, SPREAD - first)
+            spread[first] = psum.tile([P, n * CHUNK], BF16, name="spread", tag="f_bank1" if first else "detour")
+            for i in range(n):
+                bias_matmul(spread[first][:, i * CHUNK : (i + 1) * CHUNK], first + i, True)
+
+        def empty_spread(first):
+            width = spread[first].shape[1]
+            nc.scalar.copy(out=bias_all[:, first * CHUNK : first * CHUNK + width], in_=spread[first][:])
 
         def widen(j):
-            wide[j] = keep.tile([P, D], BF16, name="wide", tag="wide%d" % (j % 3))
+            wide[j] = keep.tile([P, D], BF16, name="wide", tag="wide%d" % (j % 6))
             if j < VEC_WIDENS:
-                nc.vector.tensor_copy(out=wide[j][:], in_=h_raw[j][:].bitcast(FP8))
+                nc.vector.tensor_copy(out=wide[j][:], in_=h_raw[:, j, :].bitcast(FP8))
             else:
-                nc.scalar.copy(out=wide[j][:], in_=h_raw[j][:].bitcast(FP8))
+                nc.scalar.copy(out=wide[j][:], in_=h_raw[:, j, :].bitcast(FP8))
 
         def turn(j):
             turned[j] = next_bank([P, 2, GROUPS, P], F32)
@@ -267,14 +267,14 @@ def tile_previewramprefinedvocablogits_w8_kernel(
             nc.scalar.activation(out=parts[:], in_=sums[j][:], func=ACT.Copy, scale=-1.0 / V, accum_out=neg_mu[j][:])
             ramp[j] = keep.tile([P, V], F32, name="ramp", tag="ramp%d" % (j % 4))
 
-        def rectify(j, half):
-            cols = slice(half * HALF, (half + 1) * HALF)
+        def rectify(j, first, stop):
+            cols = slice(first * CHUNK, stop * CHUNK)
             nc.scalar.activation(out=ramp[j][:, cols], in_=prev[j][:, cols], func=ACT.Relu, bias=neg_mu[j][:])
 
-        def weigh(j, c):
-            cols = slice(c * CHUNK, (c + 1) * CHUNK)
+        def weigh(j, c, lo=0, hi=CHUNK):
+            cols = slice(c * CHUNK + lo, c * CHUNK + hi)
             nc.vector.scalar_tensor_tensor(
-                out=ramp[j][:, cols], in0=ramp[j][:, cols], scalar=1.0, in1=banks[1, j, c][:],
+                out=ramp[j][:, cols], in0=ramp[j][:, cols], scalar=1.0, in1=banks[1, j, c][:, lo:hi],
                 op0=ALU.min, op1=ALU.mult,
             )
 
@@ -286,99 +286,139 @@ def tile_previewramprefinedvocablogits_w8_kernel(
         turn(0)
         widen(1)
         turn(1)
-        permute_words(0)
         widen(2)
-        spread_bias()
+        widen(3)
+        widen(4)
+        spread_bias(0)
+        spread_bias(2)
+        empty_spread(2)
+        empty_spread(0)
         scale_h(0)
-        permute_scales(0)
+        permute_words(0)
         quantize(-4, 0, H_COLS)
+        permute_scales(0)
         project(0, 0)
         round_f(0, 0)
         turn(2)
-        widen(3)
+        widen(5)
         scale_h(1)
         permute_words(1)
         quantize(-3, 0, H_COLS)
         permute_scales(1)
-        quantize(-2, H_COLS, H_COLS + P)
+        quantize(-3, H_COLS, H_COLS + P)
         project(1, 0)
-        project(0, 1)
         round_f(1, 0)
-        round_f(0, 1)
         logits_turned(0)
         park_turned(0)
         logits(0, 0, 2)
-        project(1, 1)
+        project(0, 1)
+        round_f(0, 1)
         logits(0, 0, 0)
         logits(0, 0, 1)
         scale_h(2)
-        quantize(-1, H_COLS, H_COLS + P)
+        quantize(-2, H_COLS, H_COLS + P)
         quantize(-2, 0, H_COLS)
-        quantize(-2, H_COLS + P, 2 * H_COLS)
         turn_back(0)
         turn(3)
-        round_f(1, 1)
+        project(2, 0)
         empty_back(0)
-        for c in (2, 0, 1):
-            add_bias(0, c)
-        row_mean(0)
-        rectify(0, 0)
-        widen(4)
-        quantize(-1, H_COLS + P, 2 * H_COLS)
-        scale_h(3)
+        add_bias(0, 2)
+        quantize(-3, H_COLS + P, 2 * H_COLS)
+        add_bias(0, 0)
+        add_bias(0, 1)
         logits(1, 0, 0)
         logits(1, 0, 1)
-        project(2, 0)
-        project(2, 1)
+        logits_turned(1)
+        project(1, 1)
+        row_mean(0)
+        rectify(0, 0, 1)
+        rectify(0, 1, 2)
+        park_turned(1)
+        scale_h(3)
+        for c in range(SPREAD):
+            logits(0, 1, c)
 
         last = TILES - 1
         for s in range(TILES):
             nxt = s + 1 <= last
             if nxt:
-                logits(0, s + 1, 0)
-                logits_turned(s + 1)
-                logits(0, s + 1, 1)
-                logits(0, s + 1, 2)
-            rectify(s, 1)
+                turn_back(s + 1)
+            if s == 0:
+                round_f(1, 1)
+                round_f(2, 0)
+            if s == last:
+                rectify(s, 2, 3)
+                rectify(s, 3, 4)
+            else:
+                rectify(s, 2, 4)
             weigh(s, 0)
+            if s + H_LEAD <= last:
+                turn(s + H_LEAD)
+            if s == 0:
+                project(2, 1)
             weigh(s, 1)
             if s == 0:
                 quantize(-1, 0, H_COLS)
             if s < last:
                 finish(nc.gpsimd, s, slice(0, HALF))
-            if s + H_LEAD <= last:
-                turn(s + H_LEAD)
-            if nxt:
-                park_turned(s + 1)
-                turn_back(s + 1)
-            if s + F_LEAD <= last:
-                round_f(s + F_LEAD, 0)
-                round_f(s + F_LEAD, 1)
             if nxt:
                 empty_back(s + 1)
-            logits(1, s, 2)
+            if s == 0:
+                round_f(2, 1)
+            if 0 < s < last - H_LEAD:
+                widen(s + H_LEAD + 1)
             if nxt:
                 add_bias(s + 1, 0)
-            logits(1, s, 3)
-            if s + F_LEAD + 1 <= last:
-                project(s + F_LEAD + 1, 0)
-                project(s + F_LEAD + 1, 1)
+            if s + F_LEAD <= last:
+                project(s + F_LEAD, 0)
+                round_f(s + F_LEAD, 0)
+            if s == 0:
+                logits(1, s, 2)
+                logits(1, s, 3)
+            if s + F_LEAD <= last:
+                project(s + F_LEAD, 1)
+                round_f(s + F_LEAD, 1)
+            if s > 0:
+                logits(1, s, 2)
+                logits(1, s, 3)
             if nxt:
                 add_bias(s + 1, 1)
-                logits(1, s + 1, 0)
                 add_bias(s + 1, 2)
-                logits(1, s + 1, 1)
+            if nxt:
                 row_mean(s + 1)
-                rectify(s + 1, 0)
-            if s + H_LEAD + 1 <= last:
-                widen(s + H_LEAD + 1)
+                rectify(s + 1, 0, 1)
+                rectify(s + 1, 1, 2)
             if s + H_LEAD <= last:
                 scale_h(s + H_LEAD)
+            if s == 0:
+                quantize(-2, H_COLS + P, 2 * H_COLS)
+                quantize(-1, H_COLS, 2 * H_COLS)
+            if nxt:
+                logits(1, s + 1, 0)
+                logits(1, s + 1, 1)
+            if s + 2 <= last:
+                logits_turned(s + 2)
+                park_turned(s + 2)
+            if s + 2 <= last:
+                logits(0, s + 2, 0)
             weigh(s, 2)
-            weigh(s, 3)
-            if s + F_LEAD <= last:
-                quantize(s, 0 if s + H_LEAD <= last else H_COLS, 2 * H_COLS)
-            if s < last:
+            if s + 2 <= last:
+                logits(0, s + 2, 1)
+            if s + H_LEAD < last:
+                weigh(s, 3, 0, CHUNK - 64)
+                quantize(s, 0, 2 * H_COLS)
+                weigh(s, 3, CHUNK - 64, CHUNK)
+            else:
+                weigh(s, 3)
+                if s + F_LEAD <= last:
+                    quantize(s, 0 if s + H_LEAD <= last else H_COLS, 2 * H_COLS)
+            if s + 2 <= last:
+                logits(0, s + 2, 2)
+            if s < last - 1:
                 finish(nc.gpsimd, s, slice(HALF, V))
-        for c in range(CHUNKS):
+        for c in range(CHUNKS - 2, CHUNKS):
+            finish(nc.vector, last - 1, slice(c * CHUNK, (c + 1) * CHUNK))
+        for c in range(CHUNKS - 1):
             finish(nc.vector, last, slice(c * CHUNK, (c + 1) * CHUNK))
+        finish(nc.vector, last, slice(V - CHUNK, V - CHUNK // 2))
+        finish(nc.vector, last, slice(V - CHUNK // 2, V))

from contextlib import ExitStack

import concourse.mybir as mybir
from concourse.masks import make_identity

T, D, R, V = 1024, 1024, 512, 2048
FLOPS = 2 * (2 * T * D * R + 2 * T * R * V)

F32 = mybir.dt.float32
BF16 = mybir.dt.bfloat16
I32 = mybir.dt.int32
U8 = mybir.dt.uint8
FP8 = mybir.dt.float8_e4m3fn
FP8X4 = mybir.dt.float8_e4m3fn_x4
ALU = mybir.AluOpType
ACT = mybir.ActivationFunctionType

P = 128
PACK = 4
TILES = T // P
GROUPS = D // (P * PACK)
CHUNK = 512
CHUNKS = V // CHUNK
HALF = V // 2
QUADS = 4
H_COLS = GROUPS * P
VEC_BANKS = 5
ACT_BANKS = 3
H_LEAD, F_LEAD = 4, 3
VEC_WIDENS = 2
SPREAD = CHUNKS - 1


def tile_previewramprefinedvocablogits_w8_kernel(
    tc, h_bytes, h_scale, u1_words, u1_scales, u2_words, u2_scales,
    b1_words, b1_scales, b2_words, b2_scales, bias, out,
):
    nc = tc.nc
    with ExitStack() as ctx:
        keep = ctx.enter_context(tc.tile_pool(name="keep", bufs=1))
        psum = ctx.enter_context(tc.psum_pool(name="psum", bufs=1))
        ctx.enter_context(tc.manual_schedule())

        ident = keep.tile([P, P], F32, name="ident")
        pick = keep.tile([P, CHUNKS], BF16, name="pick")
        bias_rows = keep.tile([P, CHUNK], BF16, name="bias_rows")
        bias_all = keep.tile([P, SPREAD * CHUNK], BF16, name="bias_all")
        hs = keep.tile([P, GROUPS, PACK], F32, name="hs")
        u_raw = [keep.tile([P, GROUPS, R], I32, name="u_raw%d" % w) for w in range(2)]
        zeroed = keep.tile([P, 4 * CHUNK], U8, name="zeroed", align_bytes=64)
        us_raw = [zeroed[:, w * R : (w + 1) * R] for w in range(2)]
        u_codes = [keep.tile([P, GROUPS, R], I32, name="u_codes%d" % w, align_bytes=64) for w in range(2)]
        u_planes = [keep.tile([P, R], U8, name="u_planes%d" % w, align_bytes=64) for w in range(2)]
        b_codes = [keep.tile([P, V], I32, name="b_codes%d" % w, align_bytes=64) for w in range(2)]
        b_planes = [zeroed[:, 2 * R + w * CHUNK : 2 * R + (w + 1) * CHUNK] for w in range(2)]
        h_raw = keep.tile([P, TILES, D], U8, name="h_raw")

        nc.vector.memset(zeroed[:].bitcast(I32), 0)
        nc.vector.memset(ident[:], 0.0)
        nc.vector.memset(bias_rows[:], 0.0)
        make_identity(nc, ident[:], nomemset=True)
        nc.scalar.copy(out=pick[:], in_=ident[:, 0:CHUNKS])

        def load_h(first, stop):
            rows = h_bytes[first * P : stop * P, :]
            nc.sync.dma_start(out=h_raw[:, first:stop, :], in_=rows.rearrange("(j p) d -> p j d", p=P))

        def load_u_scales(w, scales):
            for q in range(QUADS):
                nc.sync.dma_start(
                    out=us_raw[w][32 * q : 32 * q + 4 * GROUPS, :].bitcast(I32),
                    in_=scales[:, 4 * q : 4 * q + 4, :].bitcast(I32),
                )

        def load_u_words(w, words):
            nc.sync.dma_start(out=u_raw[w][:], in_=words.rearrange("g p n t -> p g (n t)").bitcast(I32))

        def load_b_scales(w, scales):
            for q in range(QUADS):
                nc.sync.dma_start(
                    out=b_planes[w][32 * q : 32 * q + 4 * CHUNKS, :].bitcast(I32),
                    in_=scales[0, 4 * q : 4 * q + 4, :].rearrange("j (c n) -> c j n", c=CHUNKS).bitcast(I32),
                )

        def load_b_words(w, words, half):
            cols = slice(half * HALF, (half + 1) * HALF)
            nc.sync.dma_start(out=b_codes[w][:, cols], in_=words[0].rearrange("p n t -> p (n t)").bitcast(I32)[:, cols])

        load_h(0, 1)
        nc.sync.dma_start(out=hs[:], in_=h_scale.rearrange("o (g p t) -> p (o g) t", p=P, t=PACK))
        load_h(1, 4)
        load_u_words(0, u1_words)
        load_u_scales(0, u1_scales)
        nc.sync.dma_start(out=bias_rows[0:CHUNKS, :], in_=bias.rearrange("(c n) -> c n", c=CHUNKS))
        load_h(4, 6)
        load_u_words(1, u2_words)
        load_u_scales(1, u2_scales)
        load_b_words(0, b1_words, 1)
        load_b_scales(0, b1_scales)
        load_b_words(0, b1_words, 0)
        load_b_scales(1, b2_scales)
        load_b_words(1, b2_words, 0)
        load_h(6, 8)
        load_b_words(1, b2_words, 1)

        wide, turned, f_banks, stage, codes, planes, prev, ramp, sums, banks = ({} for i in range(10))
        across, parked, back, neg_mu, spread = {}, {}, {}, {}, {}
        taken = []

        def next_bank(shape, dtype):
            taken.append(len(taken))
            return psum.tile(shape, dtype, name="bank", tag="ring%d" % (taken[-1] % VEC_BANKS))

        def stage_tiles(s):
            if s not in stage:
                stage[s] = keep.tile([P, 2 * D], BF16, name="stage", tag="stage%d" % (s % 4), align_bytes=64)
                codes[s] = keep.tile([P, 2 * H_COLS], I32, name="codes", tag="codes%d" % (s % 5), align_bytes=64)
                planes[s] = keep.tile([P, 2 * H_COLS], U8, name="planes", tag="planes%d" % (s % 5), align_bytes=64)
            return stage[s]

        def permute_scales(w):
            nc.vector.tensor_copy(
                out=u_planes[w][:].rearrange("p (t a b) -> p a t b", t=PACK, b=16),
                in_=us_raw[w][:].rearrange("p (a b t) -> p a t b", t=PACK, b=16),
            )

        def permute_words(w):
            nc.vector.tensor_copy(
                out=u_codes[w][:].rearrange("p g (t a b) -> p g a t b", t=PACK, b=4),
                in_=u_raw[w][:].rearrange("p g (a b t) -> p g a t b", t=PACK, b=4),
            )

        def bias_matmul(dst, c, stop):
            nc.tensor.matmul(
                dst, lhsT=pick[:, c : c + 1].to_broadcast([P, P]), rhs=bias_rows[:], start=True, stop=stop
            )

        def spread_bias(first):
            n = min(2, SPREAD - first)
            spread[first] = psum.tile([P, n * CHUNK], BF16, name="spread", tag="f_bank1" if first else "detour")
            for i in range(n):
                bias_matmul(spread[first][:, i * CHUNK : (i + 1) * CHUNK], first + i, True)

        def empty_spread(first):
            width = spread[first].shape[1]
            nc.scalar.copy(out=bias_all[:, first * CHUNK : first * CHUNK + width], in_=spread[first][:])

        def widen(j):
            wide[j] = keep.tile([P, D], BF16, name="wide", tag="wide%d" % (j % 6))
            if j < VEC_WIDENS:
                nc.vector.tensor_copy(out=wide[j][:], in_=h_raw[:, j, :].bitcast(FP8))
            else:
                nc.scalar.copy(out=wide[j][:], in_=h_raw[:, j, :].bitcast(FP8))

        def turn(j):
            turned[j] = next_bank([P, 2, GROUPS, P], F32)
            pairs = wide[j][:].bitcast(F32)
            for g in range(GROUPS):
                for u in range(2):
                    nc.tensor.transpose(turned[j][:, u, g, :], pairs[:, 256 * g + u : 256 * (g + 1) : 2], ident[:])

        def scale_h(j):
            dst = stage_tiles(j - H_LEAD)
            src = turned[j][:].rearrange("p u g n -> p (u g n)").bitcast(BF16)
            nc.vector.tensor_tensor(
                out=dst[:, 0:D].rearrange("p (g n u e) -> p g n u e", g=GROUPS, u=2, e=2),
                in0=src.rearrange("p (u g n e) -> p g n u e", u=2, g=GROUPS, e=2),
                in1=hs[:].rearrange("p g (u e) -> p g u e", u=2).unsqueeze(2).to_broadcast([P, GROUPS, P, 2, 2]),
                op=ALU.mult,
            )

        def quantize(s, lo, hi):
            nc.vector.quantize_mx(
                out=codes[s][:, lo:hi].bitcast(FP8X4),
                scales=planes[s][:, lo:hi],
                in_=stage[s][:, PACK * lo : PACK * hi],
            )

        def project(j, w):
            bank = psum.tile([P, PACK, P], F32, name="f_bank", tag="f_bank%d" % w)
            f_banks[j, w] = bank
            for t in range(PACK):
                cols = slice(t * P, (t + 1) * P)
                for g in range(GROUPS):
                    nc.tensor.matmul_mx(
                        out=bank[:, t, :],
                        lhsT=u_codes[w][:, g, cols].bitcast(FP8X4),
                        lhsT_scale=u_planes[w][4 * g :, cols],
                        rhs=codes[j - H_LEAD][:, g * P : (g + 1) * P].bitcast(FP8X4),
                        rhs_scale=planes[j - H_LEAD][:, g * P : (g + 1) * P],
                        start=(g == 0),
                        stop=(g == GROUPS - 1),
                    )

        def round_f(j, w):
            dst = stage_tiles(j - F_LEAD)
            nc.scalar.copy(
                out=dst[:, D + w * R : D + (w + 1) * R].rearrange("p (n t) -> p n t", t=PACK),
                in_=f_banks[j, w][:].rearrange("p t n -> p n t"),
            )

        def logits_turned(j):
            c = SPREAD
            across[j] = psum.tile([P, CHUNK], F32, name="across", tag="detour")
            cols = slice(H_COLS, H_COLS + P)
            for i in range(CHUNK // P):
                nc.tensor.matmul_mx(
                    out=across[j][:, i * P : (i + 1) * P],
                    lhsT=b_codes[0][:, c * CHUNK + i * P : c * CHUNK + (i + 1) * P].bitcast(FP8X4),
                    lhsT_scale=b_planes[0][4 * c :, i * P : (i + 1) * P],
                    rhs=codes[j - F_LEAD][:, cols].bitcast(FP8X4),
                    rhs_scale=planes[j - F_LEAD][:, cols],
                    start=True,
                    stop=True,
                )

        def park_turned(j):
            parked[j] = keep.tile([P, CHUNK], F32, name="parked", tag="parked%d" % (j % 2))
            nc.scalar.copy(out=parked[j][:], in_=across[j][:])

        def turn_back(j):
            back[j] = psum.tile([P, CHUNK], F32, name="back", tag="detour")
            bias_matmul(back[j][:], SPREAD, False)
            for i in range(CHUNK // P):
                cols = slice(i * P, (i + 1) * P)
                nc.tensor.matmul(
                    back[j][:, cols], lhsT=parked[j][:, cols], rhs=ident[:], is_transpose=True,
                    start=False, stop=(i == CHUNK // P - 1),
                )

        def preview_tiles(j):
            if j not in prev:
                prev[j] = keep.tile([P, V], F32, name="prev", tag="prev%d" % (j % 3))
                sums[j] = keep.tile([P, CHUNKS], F32, name="sums", tag="sums%d" % (j % 2))

        def empty_back(j):
            preview_tiles(j)
            nc.scalar.activation(
                out=prev[j][:, SPREAD * CHUNK :], in_=back[j][:], func=ACT.Copy,
                accum_out=sums[j][:, SPREAD : SPREAD + 1],
            )

        def logits(w, j, c):
            banks[w, j, c] = next_bank([P, CHUNK], F32)
            cols = slice(H_COLS + w * P, H_COLS + (w + 1) * P)
            nc.tensor.matmul_mx(
                out=banks[w, j, c][:],
                lhsT=codes[j - F_LEAD][:, cols].bitcast(FP8X4),
                lhsT_scale=planes[j - F_LEAD][:, cols],
                rhs=b_codes[w][:, c * CHUNK : (c + 1) * CHUNK].bitcast(FP8X4),
                rhs_scale=b_planes[w][4 * c :, :],
                start=True,
                stop=True,
            )

        def add_bias(j, c):
            preview_tiles(j)
            cols = slice(c * CHUNK, (c + 1) * CHUNK)
            nc.vector.scalar_tensor_tensor(
                out=prev[j][:, cols], in0=banks[0, j, c][:], scalar=1.0, in1=bias_all[:, cols],
                op0=ALU.mult, op1=ALU.add, accum_out=sums[j][:, c : c + 1],
            )

        def row_mean(j):
            parts = keep.tile([P, CHUNKS], F32, name="parts", tag="parts%d" % (j % 2))
            neg_mu[j] = keep.tile([P, 1], F32, name="neg_mu", tag="neg_mu%d" % (j % 2))
            nc.scalar.activation(out=parts[:], in_=sums[j][:], func=ACT.Copy, scale=-1.0 / V, accum_out=neg_mu[j][:])
            ramp[j] = keep.tile([P, V], F32, name="ramp", tag="ramp%d" % (j % 4))

        def rectify(j, first, stop):
            cols = slice(first * CHUNK, stop * CHUNK)
            nc.scalar.activation(out=ramp[j][:, cols], in_=prev[j][:, cols], func=ACT.Relu, bias=neg_mu[j][:])

        def weigh(j, c, lo=0, hi=CHUNK):
            cols = slice(c * CHUNK + lo, c * CHUNK + hi)
            nc.vector.scalar_tensor_tensor(
                out=ramp[j][:, cols], in0=ramp[j][:, cols], scalar=1.0, in1=banks[1, j, c][:, lo:hi],
                op0=ALU.min, op1=ALU.mult,
            )

        def finish(engine, j, cols):
            engine.tensor_tensor(out=ramp[j][:, cols], in0=prev[j][:, cols], in1=ramp[j][:, cols], op=ALU.add)
            nc.sync.dma_start(out=out[j * P : (j + 1) * P, cols], in_=ramp[j][:, cols])

        widen(0)
        turn(0)
        widen(1)
        turn(1)
        widen(2)
        widen(3)
        widen(4)
        spread_bias(0)
        spread_bias(2)
        empty_spread(2)
        empty_spread(0)
        scale_h(0)
        permute_words(0)
        quantize(-4, 0, H_COLS)
        permute_scales(0)
        project(0, 0)
        round_f(0, 0)
        turn(2)
        widen(5)
        scale_h(1)
        permute_words(1)
        quantize(-3, 0, H_COLS)
        permute_scales(1)
        quantize(-3, H_COLS, H_COLS + P)
        project(1, 0)
        round_f(1, 0)
        logits_turned(0)
        park_turned(0)
        logits(0, 0, 2)
        project(0, 1)
        round_f(0, 1)
        logits(0, 0, 0)
        logits(0, 0, 1)
        scale_h(2)
        quantize(-2, H_COLS, H_COLS + P)
        quantize(-2, 0, H_COLS)
        turn_back(0)
        turn(3)
        project(2, 0)
        empty_back(0)
        add_bias(0, 2)
        quantize(-3, H_COLS + P, 2 * H_COLS)
        add_bias(0, 0)
        add_bias(0, 1)
        logits(1, 0, 0)
        logits(1, 0, 1)
        logits_turned(1)
        project(1, 1)
        row_mean(0)
        rectify(0, 0, 1)
        rectify(0, 1, 2)
        park_turned(1)
        scale_h(3)
        for c in range(SPREAD):
            logits(0, 1, c)

        last = TILES - 1
        for s in range(TILES):
            nxt = s + 1 <= last
            if nxt:
                turn_back(s + 1)
            if s == 0:
                round_f(1, 1)
                round_f(2, 0)
            if s == last:
                rectify(s, 2, 3)
                rectify(s, 3, 4)
            else:
                rectify(s, 2, 4)
            weigh(s, 0)
            if s + H_LEAD <= last:
                turn(s + H_LEAD)
            if s == 0:
                project(2, 1)
            weigh(s, 1)
            if s == 0:
                quantize(-1, 0, H_COLS)
            if s < last:
                finish(nc.gpsimd, s, slice(0, HALF))
            if nxt:
                empty_back(s + 1)
            if s == 0:
                round_f(2, 1)
            if 0 < s < last - H_LEAD:
                widen(s + H_LEAD + 1)
            if nxt:
                add_bias(s + 1, 0)
            if s + F_LEAD <= last:
                project(s + F_LEAD, 0)
                round_f(s + F_LEAD, 0)
            if s == 0:
                logits(1, s, 2)
                logits(1, s, 3)
            if s + F_LEAD <= last:
                project(s + F_LEAD, 1)
                round_f(s + F_LEAD, 1)
            if s > 0:
                logits(1, s, 2)
                logits(1, s, 3)
            if nxt:
                add_bias(s + 1, 1)
                add_bias(s + 1, 2)
            if nxt:
                row_mean(s + 1)
                rectify(s + 1, 0, 1)
                rectify(s + 1, 1, 2)
            if s + H_LEAD <= last:
                scale_h(s + H_LEAD)
            if s == 0:
                quantize(-2, H_COLS + P, 2 * H_COLS)
                quantize(-1, H_COLS, 2 * H_COLS)
            if nxt:
                logits(1, s + 1, 0)
                logits(1, s + 1, 1)
            if s + 2 <= last:
                logits_turned(s + 2)
                park_turned(s + 2)
            if s + 2 <= last:
                logits(0, s + 2, 0)
            weigh(s, 2)
            if s + 2 <= last:
                logits(0, s + 2, 1)
            if s + H_LEAD < last:
                weigh(s, 3, 0, CHUNK - 64)
                quantize(s, 0, 2 * H_COLS)
                weigh(s, 3, CHUNK - 64, CHUNK)
            else:
                weigh(s, 3)
                if s + F_LEAD <= last:
                    quantize(s, 0 if s + H_LEAD <= last else H_COLS, 2 * H_COLS)
            if s + 2 <= last:
                logits(0, s + 2, 2)
            if s < last - 1:
                finish(nc.gpsimd, s, slice(HALF, V))
        for c in range(CHUNKS - 2, CHUNKS):
            finish(nc.vector, last - 1, slice(c * CHUNK, (c + 1) * CHUNK))
        for c in range(CHUNKS - 1):
            finish(nc.vector, last, slice(c * CHUNK, (c + 1) * CHUNK))
        finish(nc.vector, last, slice(V - CHUNK, V - CHUNK // 2))
        finish(nc.vector, last, slice(V - CHUNK // 2, V))
